import numpy as np
import ml_dtypes


def mxq(x, axis, fmt="e4m3"):
    dtype, down = {"e4m3": (ml_dtypes.float8_e4m3fn, 7), "e5m2": (ml_dtypes.float8_e5m2, 14)}[fmt]
    v = np.moveaxis(np.asarray(x, np.float32).astype(ml_dtypes.bfloat16).astype(np.float64), axis, -1)
    blocks = v.reshape(v.shape[:-1] + (-1, 32))
    amax = np.abs(blocks).max(-1, keepdims=True)
    byte = np.maximum(np.where(amax > 0, np.frexp(amax)[1] - 1 + 127, 0) - down, 1)
    scale = np.exp2(byte - 127.0)
    codes = (blocks / scale).astype(np.float32).astype(dtype).astype(np.float64)
    return np.moveaxis((codes * scale).reshape(v.shape), -1, axis)


WIDE = False


def mx_kscale(k):
    if not WIDE:
        return np.ones(k)
    levels = np.array([10, -10, 5, -5, 0])
    if k % 512:
        return np.exp2(np.random.permutation(np.resize(levels, k // 32))).repeat(32)
    a = np.empty((k // 512, 16))
    for p in range(k // 512):
        a[p, :8] = np.random.permutation(np.resize(levels, 8))
        for g in range(8):
            far = levels[np.abs(levels - a[p, g]) >= 10]
            a[p, g + 8] = far[np.random.randint(len(far))]
    return np.exp2(a.ravel()).repeat(32)


def f64(x):
    return np.asarray(x).astype(np.float64)


def striped(idx):
    return np.tile(np.asarray(idx).reshape(-1, 16).T, (8, 1)).astype(np.uint16)


def unstriped(offs):
    return offs[:16].T.reshape(-1).astype(np.int64)


E2M1 = np.array([0.0, 0.5, 1.0, 1.5, 2.0, 3.0, 4.0, 6.0, -0.0, -0.5, -1.0, -1.5, -2.0, -3.0, -4.0, -6.0])


def pack_weight(w, fmt):
    k, n = w.shape
    w = f64(np.asarray(w, np.float32).astype(ml_dtypes.bfloat16)).reshape(k // 32, 32, n)
    amax = np.abs(w).max(1)
    if fmt == "e4m3":
        byte = np.frexp(amax)[1] - 1 + 127 - 7
    else:
        mant, ex = np.frexp(amax / 6.0)
        byte = np.where(mant > 0.5, ex, ex - 1) + 127
    byte = np.clip(np.where(amax > 0, byte, 1), 1, 254)
    scaled = (w * np.exp2(127.0 - byte)[:, None, :]).reshape(k, n).astype(np.float32)
    by_word = np.ascontiguousarray(scaled.reshape(k // 512, 128, 4, n).transpose(0, 1, 3, 2))
    if fmt == "e4m3":
        words = by_word.astype(ml_dtypes.float8_e4m3fn).view(np.uint8)
    else:
        c = by_word.astype(ml_dtypes.float4_e2m1fn).view(np.uint8) & 0xF
        words = (c[..., 0::2] | (c[..., 1::2] << 4)).reshape(k // 512, 128, 2 * n)
    return np.ascontiguousarray(words), np.ascontiguousarray(byte.astype(np.uint8).reshape(k // 512, 16, n))


def unpack_weight(words, scales, fmt):
    g, _, n = scales.shape
    words = np.ascontiguousarray(words).reshape(g, 128, n, -1)
    if fmt == "e4m3":
        vals = words.view(ml_dtypes.float8_e4m3fn).astype(np.float64)
    else:
        nib = np.empty((g, 128, n, 4), np.uint8)
        nib[..., 0::2] = words & 0xF
        nib[..., 1::2] = words >> 4
        vals = E2M1[nib]
    vals = vals * np.repeat(np.exp2(scales.astype(np.float64) - 127.0), 8, axis=1)[..., None]
    return vals.transpose(0, 1, 3, 2).reshape(g * 512, n)


K, T, J, R, N = 512, 2048, 512, 512, 512


def setup_inputs():
    n = np.random.standard_normal
    idx = np.random.permutation(T)[:J]
    fk = mx_kscale(K)
    fr = mx_kscale(R)
    xtp = pack_weight(n((K, T)) / fk[:, None], "e4m3")
    wap = pack_weight(n((K, R)) * 1 / np.sqrt(K) * fk[:, None], "e2m1")
    wbp = pack_weight(n((R, N)) * 1 / np.sqrt(R) / fr[:, None], "e4m3")
    return {
        "xt_words": xtp[0],
        "xt_scales": xtp[1],
        "wa_words": wap[0],
        "wa_scales": wap[1],
        "us": (np.random.uniform(0.5, 2.0, (R, 1)) * fr[:, None]).astype(np.float32),
        "wb_words": wbp[0],
        "wb_scales": wbp[1],
        "rw": (np.random.uniform(0.5, 2.0, (1, J))).astype(np.float32),
        "offs": striped(idx),
    }


def reference(xt_words, xt_scales, wa_words, wa_scales, us, wb_words, wb_scales, rw, offs):
    idx = unstriped(offs)
    xtu = unpack_weight(xt_words, xt_scales, "e4m3")
    wau = unpack_weight(wa_words, wa_scales, "e2m1")
    wbu = unpack_weight(wb_words, wb_scales, "e4m3")
    xtidxg = xtu[:, idx]
    a = wau.T @ xtidxg
    hid = a / (np.mean(np.abs(a), axis=1, keepdims=True) + 0.1) * f64(us)
    hidq = mxq(hid, 0, "e4m3")
    p = wbu.T @ hidq
    y = p * f64(rw)
    return y

@@ -1,0 +1,189 @@
+from contextlib import ExitStack
+
+import concourse.mybir as mybir
+
+F32 = mybir.dt.float32
+BF16 = mybir.dt.bfloat16
+I32 = mybir.dt.int32
+U32 = mybir.dt.uint32
+U16 = mybir.dt.uint16
+U8 = mybir.dt.uint8
+FP8X4 = mybir.dt.float8_e4m3fn_x4
+FP4X4 = mybir.dt.float4_e2m1fn_x4
+ALU = mybir.AluOpType
+ACT = mybir.ActivationFunctionType
+
+P = 128
+PACK = 4
+K, T, J, R, N = 512, 2048, 512, 512, 512
+HALVES = 2
+JH = J // HALVES
+FLOPS = 2 * K * R * J + 2 * R * N * J
+
+
+def load_scale_rows(queues, plane, rows):
+    for q, queue in enumerate(queues):
+        queue.dma_start(
+            out=plane[32 * q : 32 * q + 4, :].bitcast(I32),
+            in_=rows[4 * q : 4 * q + 4, :].bitcast(I32),
+        )
+
+
+def tile_list_hidden_evened_kernel(
+    tc, xt_words, xt_scales, wa_words, wa_scales, us, wb_words, wb_scales, rw, offs, out
+):
+    nc = tc.nc
+    with ExitStack() as ctx:
+        lists = ctx.enter_context(tc.tile_pool(name="lists", bufs=1))
+        sb = ctx.enter_context(tc.tile_pool(name="sb", bufs=1))
+        reused = ctx.enter_context(tc.tile_pool(name="reused", bufs=1))
+        ps = ctx.enter_context(tc.psum_pool(name="ps", bufs=1))
+
+        offsets = lists.tile([P, J // 16], U16, name="offsets")
+        x_words = sb.tile([P, T], I32, name="x_words", align_bytes=64)
+        x_plane = sb.tile([P, T], U8, name="x_plane", tag="x_plane_then_rw", align_bytes=64)
+        wa_raw = reused.tile([P, 2 * R], U8, name="wa_raw", offset=0, align_bytes=64)
+        wa_plane_raw = reused.tile([P, R], U8, name="wa_plane_raw", offset=4096, align_bytes=64)
+
+        nc.vector.memset(x_plane[:].bitcast(I32), 0)
+        nc.gpsimd.memset(wa_plane_raw[:].bitcast(I32), 0)
+
+        nc.sync.dma_start(offsets[:], offs)
+        nc.scalar.dma_start(out=wa_raw[:].bitcast(I32), in_=wa_words[0].bitcast(I32))
+        nc.sync.dma_start(
+            out=x_words[:], in_=xt_words[0].rearrange("p n t -> p (n t)").bitcast(I32)
+        )
+        load_scale_rows([nc.scalar] * 4, x_plane, xt_scales[0])
+        load_scale_rows([nc.gpsimd, nc.gpsimd, nc.scalar, nc.scalar], wa_plane_raw, wa_scales[0])
+
+        wa_dealt = sb.tile([P, PACK, 2 * P], U8, name="wa_dealt", align_bytes=64)
+        nc.vector.tensor_copy(
+            out=wa_dealt[:].bitcast(U16),
+            in_=wa_raw[:].bitcast(U16).rearrange("p (q t) -> p t q", t=PACK),
+        )
+        xg_plane = sb.tile([P, J], U8, name="xg_plane", align_bytes=64)
+        nc.vector.tensor_copy(xg_plane[:], x_plane[:].indirect(offsets[:]))
+        wa_plane = sb.tile([P, PACK, P], U8, name="wa_plane", align_bytes=64)
+        nc.vector.tensor_copy(
+            out=wa_plane[:], in_=wa_plane_raw[:].rearrange("p (q t) -> p t q", t=PACK)
+        )
+
+        us_cols = reused.tile([P, PACK], F32, name="us_cols", offset=0, align_bytes=64)
+        nc.sync.dma_start(out=us_cols[:], in_=us.rearrange("(p t) o -> p (t o)", t=PACK))
+        wb_codes = reused.tile([P, PACK * N], U8, name="wb_codes", offset=640, align_bytes=64)
+        wb_plane = reused.tile([P, N], U8, name="wb_plane", offset=64, align_bytes=64)
+        nc.gpsimd.memset(wb_plane[:].bitcast(I32), 0)
+        nc.sync.dma_start(
+            out=wb_codes[:].bitcast(I32),
+            in_=wb_words[0].rearrange("p n t -> p (n t)").bitcast(I32),
+        )
+        load_scale_rows([nc.sync] * 4, wb_plane, wb_scales[0])
+
+        rw_rows = sb.tile([P, J], F32, name="rw_rows", tag="x_plane_then_rw", align_bytes=64)
+        nc.sync.dma_start(out=rw_rows[:], in_=rw[0].partition_broadcast(P))
+
+        xg_words = []
+        for h in range(HALVES):
+            gathered = reused.tile(
+                [P, JH], U32, name=f"xg_words{h}", offset=4096 + 4 * JH * (1 - h), align_bytes=64
+            )
+            cols = slice(h * JH // 16, (h + 1) * JH // 16)
+            nc.vector.tensor_copy(gathered[:], x_words[:].bitcast(U32).indirect(offsets[:, cols]))
+            xg_words.append(gathered)
+
+        pairs = [
+            sb.tile([P, 2, JH, 2], BF16, name=f"pairs{h}", align_bytes=64) for h in range(HALVES)
+        ]
+        a_banks = {}
+        factors = []
+        for u in range(2):
+            parts = sb.tile([P, HALVES, 2], F32, name=f"parts{u}")
+            for h in range(HALVES):
+                bank = ps.tile([P, 2, JH], F32, name=f"a{h}{u}", tag=f"bank{2 * u + h}")
+                for e in range(2):
+                    t = 2 * u + e
+                    nc.tensor.matmul_mx(
+                        out=bank[:, e, :],
+                        lhsT=wa_dealt[:, t, :].bitcast(FP4X4),
+                        lhsT_scale=wa_plane[:, t, :],
+                        rhs=xg_words[h][:].bitcast(FP8X4),
+                        rhs_scale=xg_plane[:, h * JH : (h + 1) * JH],
+                        start=True,
+                        stop=True,
+                    )
+                for e in range(2):
+                    magnitudes = sb.tile([P, JH], BF16, name=f"magnitudes{h}{u}{e}")
+                    nc.scalar.activation(
+                        magnitudes[:],
+                        bank[:, e, :],
+                        ACT.Abs,
+                        scale=1.0 / J,
+                        accum_out=parts[:, h, e : e + 1],
+                    )
+                a_banks[h, u] = bank
+            divisor = sb.tile([P, 2], F32, name=f"divisor{u}")
+            nc.vector.scalar_tensor_tensor(
+                divisor[:], parts[:, 0, :], 0.1, parts[:, 1, :], ALU.add, ALU.add
+            )
+            inverse = sb.tile([P, 2], F32, name=f"inverse{u}")
+            nc.vector.reciprocal(inverse[:], divisor[:])
+            factor = sb.tile([P, 2], F32, name=f"factor{u}")
+            nc.vector.tensor_tensor(factor[:], inverse[:], us_cols[:, 2 * u : 2 * u + 2], ALU.mult)
+            factors.append(factor)
+        for u in range(2):
+            for h in range(HALVES):
+                nc.vector.tensor_tensor(
+                    pairs[h][:, u, :, :],
+                    a_banks[h, u][:].rearrange("p e j -> p j e"),
+                    factors[u][:].unsqueeze(1).to_broadcast([P, JH, 2]),
+                    ALU.mult,
+                )
+
+        woven = []
+        for h in range(HALVES):
+            tile = sb.tile([P, JH, PACK], BF16, name=f"woven{h}", align_bytes=64)
+            nc.vector.tensor_copy(
+                out=tile[:].bitcast(F32),
+                in_=pairs[h][:].bitcast(F32).rearrange("p u j o -> p j (u o)"),
+            )
+            woven.append(tile)
+        hid = []
+        for h in range(HALVES):
+            codes = sb.tile([P, JH], U32, name=f"hid_codes{h}", align_bytes=64)
+            plane = sb.tile([P, JH], U8, name=f"hid_plane{h}", align_bytes=64)
+            nc.vector.quantize_mx(
+                out=codes[:].bitcast(FP8X4),
+                scales=plane[:],
+                in_=woven[h][:].rearrange("p j t -> p (j t)"),
+            )
+            hid.append((codes, plane))
+
+        for h in range(HALVES):
+            codes, plane = hid[h]
+            for pair in range(2):
+                bank = ps.tile([P, 2, JH], F32, name=f"p{h}{pair}", tag=f"bank{4 + 2 * h + pair}")
+                for b in range(2):
+                    n0 = (2 * pair + b) * P
+                    nc.tensor.matmul_mx(
+                        out=bank[:, b, :],
+                        lhsT=wb_codes[:, PACK * n0 : PACK * (n0 + P)].bitcast(FP8X4),
+                        lhsT_scale=wb_plane[:, n0 : n0 + P],
+                        rhs=codes[:].bitcast(FP8X4),
+                        rhs_scale=plane[:],
+                        start=True,
+                        stop=True,
+                    )
+                result = sb.tile([P, 2, JH], F32, name=f"result{h}{pair}")
+                j_cols = slice(h * JH, (h + 1) * JH)
+                nc.vector.tensor_tensor(
+                    result[:],
+                    bank[:],
+                    rw_rows[:, j_cols].unsqueeze(1).to_broadcast([P, 2, JH]),
+                    ALU.mult,
+                )
+                nc.sync.dma_start(
+                    out=out[2 * pair * P : 2 * (pair + 1) * P, j_cols].rearrange(
+                        "(b p) j -> p b j", p=P
+                    ),
+                    in_=result[:],
+                )

@@ -18,6 +18,7 @@ PACK = 4
 K, T, J, R, N = 512, 2048, 512, 512, 512
 HALVES = 2
 JH = J // HALVES
+JQ = JH // 2
 FLOPS = 2 * K * R * J + 2 * R * N * J
 
 
@@ -61,12 +62,26 @@ def tile_list_hidden_evened_kernel(
             out=wa_dealt[:].bitcast(U16),
             in_=wa_raw[:].bitcast(U16).rearrange("p (q t) -> p t q", t=PACK),
         )
-        xg_plane = sb.tile([P, J], U8, name="xg_plane", align_bytes=64)
-        nc.vector.tensor_copy(xg_plane[:], x_plane[:].indirect(offsets[:]))
-        wa_plane = sb.tile([P, PACK, P], U8, name="wa_plane", align_bytes=64)
-        nc.vector.tensor_copy(
-            out=wa_plane[:], in_=wa_plane_raw[:].rearrange("p (q t) -> p t q", t=PACK)
-        )
+        xg_words = []
+        xg_planes = []
+        wa_planes = []
+        for h in range(HALVES):
+            cols = slice(h * JH // 16, (h + 1) * JH // 16)
+            base = 4096 + 2048 * (1 - h)
+            plane = reused.tile([P, JH], U8, name=f"xg_plane{h}", offset=base, align_bytes=64)
+            nc.vector.tensor_copy(plane[:], x_plane[:].indirect(offsets[:, cols]))
+            words = reused.tile(
+                [P, JH], U32, name=f"xg_words{h}", offset=base + JH, align_bytes=64
+            )
+            nc.vector.tensor_copy(words[:], x_words[:].bitcast(U32).indirect(offsets[:, cols]))
+            xg_planes.append(plane)
+            xg_words.append(words)
+            if h == 0:
+                for u in range(2):
+                    dealt = sb.tile([P, 2, P], U8, name=f"wa_plane{u}", align_bytes=64)
+                    by_t = wa_plane_raw[:].rearrange("p (q t) -> p t q", t=PACK)
+                    nc.vector.tensor_copy(out=dealt[:], in_=by_t[:, 2 * u : 2 * u + 2, :])
+                    wa_planes.append(dealt)
 
         us_cols = reused.tile([P, PACK], F32, name="us_cols", offset=0, align_bytes=64)
         nc.sync.dma_start(out=us_cols[:], in_=us.rearrange("(p t) o -> p (t o)", t=PACK))
@@ -82,32 +97,23 @@ def tile_list_hidden_evened_kernel(
         rw_rows = sb.tile([P, J], F32, name="rw_rows", tag="x_plane_then_rw", align_bytes=64)
         nc.sync.dma_start(out=rw_rows[:], in_=rw[0].partition_broadcast(P))
 
-        xg_words = []
-        for h in range(HALVES):
-            gathered = reused.tile(
-                [P, JH], U32, name=f"xg_words{h}", offset=4096 + 4 * JH * (1 - h), align_bytes=64
-            )
-            cols = slice(h * JH // 16, (h + 1) * JH // 16)
-            nc.vector.tensor_copy(gathered[:], x_words[:].bitcast(U32).indirect(offsets[:, cols]))
-            xg_words.append(gathered)
+        us_inverse = sb.tile([P, PACK], F32, name="us_inverse")
+        nc.vector.reciprocal(us_inverse[:], us_cols[:])
 
-        pairs = [
-            sb.tile([P, 2, JH, 2], BF16, name=f"pairs{h}", align_bytes=64) for h in range(HALVES)
-        ]
         a_banks = {}
+        parts = [sb.tile([P, HALVES, 2], F32, name=f"parts{u}") for u in range(2)]
+        first_parts = []
         factors = []
-        for u in range(2):
-            parts = sb.tile([P, HALVES, 2], F32, name=f"parts{u}")
-            for h in range(HALVES):
-                bank = ps.tile([P, 2, JH], F32, name=f"a{h}{u}", tag=f"bank{2 * u + h}")
+        for h in range(HALVES):
+            for u in range(2):
+                bank = ps.tile([P, 2, JH], F32, name=f"a{h}{u}", tag=f"bank{2 * h + u}")
                 for e in range(2):
-                    t = 2 * u + e
                     nc.tensor.matmul_mx(
                         out=bank[:, e, :],
-                        lhsT=wa_dealt[:, t, :].bitcast(FP4X4),
-                        lhsT_scale=wa_plane[:, t, :],
+                        lhsT=wa_dealt[:, 2 * u + e, :].bitcast(FP4X4),
+                        lhsT_scale=wa_planes[u][:, e, :],
                         rhs=xg_words[h][:].bitcast(FP8X4),
-                        rhs_scale=xg_plane[:, h * JH : (h + 1) * JH],
+                        rhs_scale=xg_planes[h][:],
                         start=True,
                         stop=True,
                     )
@@ -118,72 +124,95 @@ def tile_list_hidden_evened_kernel(
                         bank[:, e, :],
                         ACT.Abs,
                         scale=1.0 / J,
-                        accum_out=parts[:, h, e : e + 1],
+                        accum_out=parts[u][:, h, e : e + 1],
                     )
                 a_banks[h, u] = bank
-            divisor = sb.tile([P, 2], F32, name=f"divisor{u}")
-            nc.vector.scalar_tensor_tensor(
-                divisor[:], parts[:, 0, :], 0.1, parts[:, 1, :], ALU.add, ALU.add
-            )
-            inverse = sb.tile([P, 2], F32, name=f"inverse{u}")
-            nc.vector.reciprocal(inverse[:], divisor[:])
-            factor = sb.tile([P, 2], F32, name=f"factor{u}")
-            nc.vector.tensor_tensor(factor[:], inverse[:], us_cols[:, 2 * u : 2 * u + 2], ALU.mult)
-            factors.append(factor)
+                if h == 0:
+                    first_part = sb.tile([P, 2], F32, name=f"first_part{u}")
+                    nc.vector.tensor_scalar(first_part[:], parts[u][:, 0, :], 0.1, None, ALU.add)
+                    first_parts.append(first_part)
+                else:
+                    divisor = sb.tile([P, 2], F32, name=f"divisor{u}")
+                    factor = sb.tile([P, 2], F32, name=f"factor{u}")
+                    for e in range(2):
+                        t = 2 * u + e
+                        nc.vector.tensor_scalar(
+                            divisor[:, e : e + 1],
+                            parts[u][:, 1, e : e + 1],
+                            first_parts[u][:, e : e + 1],
+                            us_inverse[:, t : t + 1],
+                            ALU.add,
+                            ALU.mult,
+                        )
+                        nc.vector.reciprocal(factor[:, e : e + 1], divisor[:, e : e + 1])
+                    factors.append(factor)
+
+        pieces = [(0, JQ), (JQ, JQ), (JH, JH)]
+        pairs = [
+            sb.tile([P, 2, width, 2], BF16, name=f"pairs{i}", align_bytes=64)
+            for i, (j0, width) in enumerate(pieces)
+        ]
         for u in range(2):
-            for h in range(HALVES):
+            for q in range(2):
                 nc.vector.tensor_tensor(
-                    pairs[h][:, u, :, :],
-                    a_banks[h, u][:].rearrange("p e j -> p j e"),
-                    factors[u][:].unsqueeze(1).to_broadcast([P, JH, 2]),
+                    pairs[q][:, u, :, :],
+                    a_banks[0, u][:, :, q * JQ : (q + 1) * JQ].rearrange("p e j -> p j e"),
+                    factors[u][:].unsqueeze(1).to_broadcast([P, JQ, 2]),
                     ALU.mult,
+                )
+            for e in range(2):
+                nc.scalar.activation(
+                    pairs[2][:, u, :, e],
+                    a_banks[1, u][:, e, :],
+                    ACT.Copy,
+                    scale=factors[u][:, e : e + 1],
                 )
 
         woven = []
-        for h in range(HALVES):
-            tile = sb.tile([P, JH, PACK], BF16, name=f"woven{h}", align_bytes=64)
-            nc.vector.tensor_copy(
-                out=tile[:].bitcast(F32),
-                in_=pairs[h][:].bitcast(F32).rearrange("p u j o -> p j (u o)"),
-            )
+        for i, (j0, width) in enumerate(pieces):
+            tile = sb.tile([P, width, PACK], BF16, name=f"woven{i}", align_bytes=64)
+            words_in = pairs[i][:].bitcast(F32).rearrange("p u j o -> p j (u o)")
+            if i < 2:
+                nc.vector.tensor_copy(out=tile[:].bitcast(F32), in_=words_in)
+            else:
+                nc.scalar.copy(out=tile[:].bitcast(F32), in_=words_in)
             woven.append(tile)
         hid = []
-        for h in range(HALVES):
-            codes = sb.tile([P, JH], U32, name=f"hid_codes{h}", align_bytes=64)
-            plane = sb.tile([P, JH], U8, name=f"hid_plane{h}", align_bytes=64)
+        for i, (j0, width) in enumerate(pieces):
+            codes = sb.tile([P, width], U32, name=f"hid_codes{i}", align_bytes=64)
+            plane = sb.tile([P, width], U8, name=f"hid_plane{i}", align_bytes=64)
             nc.vector.quantize_mx(
                 out=codes[:].bitcast(FP8X4),
                 scales=plane[:],
-                in_=woven[h][:].rearrange("p j t -> p (j t)"),
+                in_=woven[i][:].rearrange("p j t -> p (j t)"),
             )
             hid.append((codes, plane))
 
-        for h in range(HALVES):
-            codes, plane = hid[h]
-            for pair in range(2):
-                bank = ps.tile([P, 2, JH], F32, name=f"p{h}{pair}", tag=f"bank{4 + 2 * h + pair}")
-                for b in range(2):
-                    n0 = (2 * pair + b) * P
-                    nc.tensor.matmul_mx(
-                        out=bank[:, b, :],
-                        lhsT=wb_codes[:, PACK * n0 : PACK * (n0 + P)].bitcast(FP8X4),
-                        lhsT_scale=wb_plane[:, n0 : n0 + P],
-                        rhs=codes[:].bitcast(FP8X4),
-                        rhs_scale=plane[:],
-                        start=True,
-                        stop=True,
-                    )
-                result = sb.tile([P, 2, JH], F32, name=f"result{h}{pair}")
-                j_cols = slice(h * JH, (h + 1) * JH)
-                nc.vector.tensor_tensor(
-                    result[:],
-                    bank[:],
-                    rw_rows[:, j_cols].unsqueeze(1).to_broadcast([P, 2, JH]),
-                    ALU.mult,
+        units = [(0, 0, 2), (0, 2, 2), (1, 0, 4), (2, 0, 2), (2, 2, 1), (2, 3, 1)]
+        for k, (i, b0, blocks) in enumerate(units):
+            j0, width = pieces[i]
+            codes, plane = hid[i]
+            bank = ps.tile([P, blocks, width], F32, name=f"p{k}", tag=f"bank{(4 + k) % 8}")
+            for b in range(blocks):
+                n0 = (b0 + b) * P
+                nc.tensor.matmul_mx(
+                    out=bank[:, b, :],
+                    lhsT=wb_codes[:, PACK * n0 : PACK * (n0 + P)].bitcast(FP8X4),
+                    lhsT_scale=wb_plane[:, n0 : n0 + P],
+                    rhs=codes[:].bitcast(FP8X4),
+                    rhs_scale=plane[:],
+                    start=True,
+                    stop=True,
                 )
-                nc.sync.dma_start(
-                    out=out[2 * pair * P : 2 * (pair + 1) * P, j_cols].rearrange(
-                        "(b p) j -> p b j", p=P
-                    ),
-                    in_=result[:],
-                )
+            result = sb.tile([P, blocks, width], F32, name=f"result{k}")
+            j_cols = slice(j0, j0 + width)
+            nc.vector.tensor_tensor(
+                result[:],
+                bank[:],
+                rw_rows[:, j_cols].unsqueeze(1).to_broadcast([P, blocks, width]),
+                ALU.mult,
+            )
+            nc.sync.dma_start(
+                out=out[b0 * P : (b0 + blocks) * P, j_cols].rearrange("(b p) j -> p b j", p=P),
+                in_=result[:],
+            )

@@ -188,7 +188,7 @@ def tile_list_hidden_evened_kernel(
             )
             hid.append((codes, plane))
 
-        units = [(0, 0, 2), (0, 2, 2), (1, 0, 4), (2, 0, 2), (2, 2, 1), (2, 3, 1)]
+        units = [(0, 0, 2), (0, 2, 2), (1, 0, 2), (1, 2, 2), (2, 0, 1), (2, 1, 1), (2, 2, 1), (2, 3, 1)]
         for k, (i, b0, blocks) in enumerate(units):
             j0, width = pieces[i]
             codes, plane = hid[i]

from contextlib import ExitStack

import concourse.mybir as mybir

F32 = mybir.dt.float32
BF16 = mybir.dt.bfloat16
I32 = mybir.dt.int32
U32 = mybir.dt.uint32
U16 = mybir.dt.uint16
U8 = mybir.dt.uint8
FP8X4 = mybir.dt.float8_e4m3fn_x4
FP4X4 = mybir.dt.float4_e2m1fn_x4
ALU = mybir.AluOpType
ACT = mybir.ActivationFunctionType

P = 128
PACK = 4
K, T, J, R, N = 512, 2048, 512, 512, 512
HALVES = 2
JH = J // HALVES
JQ = JH // 2
FLOPS = 2 * K * R * J + 2 * R * N * J


def load_scale_rows(queues, plane, rows):
    for q, queue in enumerate(queues):
        queue.dma_start(
            out=plane[32 * q : 32 * q + 4, :].bitcast(I32),
            in_=rows[4 * q : 4 * q + 4, :].bitcast(I32),
        )


def tile_list_hidden_evened_kernel(
    tc, xt_words, xt_scales, wa_words, wa_scales, us, wb_words, wb_scales, rw, offs, out
):
    nc = tc.nc
    with ExitStack() as ctx:
        lists = ctx.enter_context(tc.tile_pool(name="lists", bufs=1))
        sb = ctx.enter_context(tc.tile_pool(name="sb", bufs=1))
        reused = ctx.enter_context(tc.tile_pool(name="reused", bufs=1))
        ps = ctx.enter_context(tc.psum_pool(name="ps", bufs=1))

        offsets = lists.tile([P, J // 16], U16, name="offsets")
        x_words = sb.tile([P, T], I32, name="x_words", align_bytes=64)
        x_plane = sb.tile([P, T], U8, name="x_plane", tag="x_plane_then_rw", align_bytes=64)
        wa_raw = reused.tile([P, 2 * R], U8, name="wa_raw", offset=0, align_bytes=64)
        wa_plane_raw = reused.tile([P, R], U8, name="wa_plane_raw", offset=4096, align_bytes=64)

        nc.vector.memset(x_plane[:].bitcast(I32), 0)
        nc.gpsimd.memset(wa_plane_raw[:].bitcast(I32), 0)

        nc.sync.dma_start(offsets[:], offs)
        nc.scalar.dma_start(out=wa_raw[:].bitcast(I32), in_=wa_words[0].bitcast(I32))
        nc.sync.dma_start(
            out=x_words[:], in_=xt_words[0].rearrange("p n t -> p (n t)").bitcast(I32)
        )
        load_scale_rows([nc.scalar] * 4, x_plane, xt_scales[0])
        load_scale_rows([nc.gpsimd, nc.gpsimd, nc.scalar, nc.scalar], wa_plane_raw, wa_scales[0])

        wa_dealt = sb.tile([P, PACK, 2 * P], U8, name="wa_dealt", align_bytes=64)
        nc.vector.tensor_copy(
            out=wa_dealt[:].bitcast(U16),
            in_=wa_raw[:].bitcast(U16).rearrange("p (q t) -> p t q", t=PACK),
        )
        xg_words = []
        xg_planes = []
        wa_planes = []
        for h in range(HALVES):
            cols = slice(h * JH // 16, (h + 1) * JH // 16)
            base = 4096 + 2048 * (1 - h)
            plane = reused.tile([P, JH], U8, name=f"xg_plane{h}", offset=base, align_bytes=64)
            nc.vector.tensor_copy(plane[:], x_plane[:].indirect(offsets[:, cols]))
            words = reused.tile(
                [P, JH], U32, name=f"xg_words{h}", offset=base + JH, align_bytes=64
            )
            nc.vector.tensor_copy(words[:], x_words[:].bitcast(U32).indirect(offsets[:, cols]))
            xg_planes.append(plane)
            xg_words.append(words)
            if h == 0:
                for u in range(2):
                    dealt = sb.tile([P, 2, P], U8, name=f"wa_plane{u}", align_bytes=64)
                    by_t = wa_plane_raw[:].rearrange("p (q t) -> p t q", t=PACK)
                    nc.vector.tensor_copy(out=dealt[:], in_=by_t[:, 2 * u : 2 * u + 2, :])
                    wa_planes.append(dealt)

        us_cols = reused.tile([P, PACK], F32, name="us_cols", offset=0, align_bytes=64)
        nc.sync.dma_start(out=us_cols[:], in_=us.rearrange("(p t) o -> p (t o)", t=PACK))
        wb_codes = reused.tile([P, PACK * N], U8, name="wb_codes", offset=640, align_bytes=64)
        wb_plane = reused.tile([P, N], U8, name="wb_plane", offset=64, align_bytes=64)
        nc.gpsimd.memset(wb_plane[:].bitcast(I32), 0)
        nc.sync.dma_start(
            out=wb_codes[:].bitcast(I32),
            in_=wb_words[0].rearrange("p n t -> p (n t)").bitcast(I32),
        )
        load_scale_rows([nc.sync] * 4, wb_plane, wb_scales[0])

        rw_rows = sb.tile([P, J], F32, name="rw_rows", tag="x_plane_then_rw", align_bytes=64)
        nc.sync.dma_start(out=rw_rows[:], in_=rw[0].partition_broadcast(P))

        us_inverse = sb.tile([P, PACK], F32, name="us_inverse")
        nc.vector.reciprocal(us_inverse[:], us_cols[:])

        a_banks = {}
        parts = [sb.tile([P, HALVES, 2], F32, name=f"parts{u}") for u in range(2)]
        first_parts = []
        factors = []
        for h in range(HALVES):
            for u in range(2):
                bank = ps.tile([P, 2, JH], F32, name=f"a{h}{u}", tag=f"bank{2 * h + u}")
                for e in range(2):
                    nc.tensor.matmul_mx(
                        out=bank[:, e, :],
                        lhsT=wa_dealt[:, 2 * u + e, :].bitcast(FP4X4),
                        lhsT_scale=wa_planes[u][:, e, :],
                        rhs=xg_words[h][:].bitcast(FP8X4),
                        rhs_scale=xg_planes[h][:],
                        start=True,
                        stop=True,
                    )
                for e in range(2):
                    magnitudes = sb.tile([P, JH], BF16, name=f"magnitudes{h}{u}{e}")
                    nc.scalar.activation(
                        magnitudes[:],
                        bank[:, e, :],
                        ACT.Abs,
                        scale=1.0 / J,
                        accum_out=parts[u][:, h, e : e + 1],
                    )
                a_banks[h, u] = bank
                if h == 0:
                    first_part = sb.tile([P, 2], F32, name=f"first_part{u}")
                    nc.vector.tensor_scalar(first_part[:], parts[u][:, 0, :], 0.1, None, ALU.add)
                    first_parts.append(first_part)
                else:
                    divisor = sb.tile([P, 2], F32, name=f"divisor{u}")
                    factor = sb.tile([P, 2], F32, name=f"factor{u}")
                    for e in range(2):
                        t = 2 * u + e
                        nc.vector.tensor_scalar(
                            divisor[:, e : e + 1],
                            parts[u][:, 1, e : e + 1],
                            first_parts[u][:, e : e + 1],
                            us_inverse[:, t : t + 1],
                            ALU.add,
                            ALU.mult,
                        )
                        nc.vector.reciprocal(factor[:, e : e + 1], divisor[:, e : e + 1])
                    factors.append(factor)

        pieces = [(0, JQ), (JQ, JQ), (JH, JH)]
        pairs = [
            sb.tile([P, 2, width, 2], BF16, name=f"pairs{i}", align_bytes=64)
            for i, (j0, width) in enumerate(pieces)
        ]
        for u in range(2):
            for q in range(2):
                nc.vector.tensor_tensor(
                    pairs[q][:, u, :, :],
                    a_banks[0, u][:, :, q * JQ : (q + 1) * JQ].rearrange("p e j -> p j e"),
                    factors[u][:].unsqueeze(1).to_broadcast([P, JQ, 2]),
                    ALU.mult,
                )
            for e in range(2):
                nc.scalar.activation(
                    pairs[2][:, u, :, e],
                    a_banks[1, u][:, e, :],
                    ACT.Copy,
                    scale=factors[u][:, e : e + 1],
                )

        woven = []
        for i, (j0, width) in enumerate(pieces):
            tile = sb.tile([P, width, PACK], BF16, name=f"woven{i}", align_bytes=64)
            words_in = pairs[i][:].bitcast(F32).rearrange("p u j o -> p j (u o)")
            if i < 2:
                nc.vector.tensor_copy(out=tile[:].bitcast(F32), in_=words_in)
            else:
                nc.scalar.copy(out=tile[:].bitcast(F32), in_=words_in)
            woven.append(tile)
        hid = []
        for i, (j0, width) in enumerate(pieces):
            codes = sb.tile([P, width], U32, name=f"hid_codes{i}", align_bytes=64)
            plane = sb.tile([P, width], U8, name=f"hid_plane{i}", align_bytes=64)
            nc.vector.quantize_mx(
                out=codes[:].bitcast(FP8X4),
                scales=plane[:],
                in_=woven[i][:].rearrange("p j t -> p (j t)"),
            )
            hid.append((codes, plane))

        units = [(0, 0, 2), (0, 2, 2), (1, 0, 2), (1, 2, 2), (2, 0, 1), (2, 1, 1), (2, 2, 1), (2, 3, 1)]
        for k, (i, b0, blocks) in enumerate(units):
            j0, width = pieces[i]
            codes, plane = hid[i]
            bank = ps.tile([P, blocks, width], F32, name=f"p{k}", tag=f"bank{(4 + k) % 8}")
            for b in range(blocks):
                n0 = (b0 + b) * P
                nc.tensor.matmul_mx(
                    out=bank[:, b, :],
                    lhsT=wb_codes[:, PACK * n0 : PACK * (n0 + P)].bitcast(FP8X4),
                    lhsT_scale=wb_plane[:, n0 : n0 + P],
                    rhs=codes[:].bitcast(FP8X4),
                    rhs_scale=plane[:],
                    start=True,
                    stop=True,
                )
            result = sb.tile([P, blocks, width], F32, name=f"result{k}")
            j_cols = slice(j0, j0 + width)
            nc.vector.tensor_tensor(
                result[:],
                bank[:],
                rw_rows[:, j_cols].unsqueeze(1).to_broadcast([P, blocks, width]),
                ALU.mult,
            )
            nc.sync.dma_start(
                out=out[b0 * P : (b0 + blocks) * P, j_cols].rearrange("(b p) j -> p b j", p=P),
                in_=result[:],
            )
